import numpy as np
import ml_dtypes


def mxq(x, axis, fmt="e4m3"):
    dtype, down = {"e4m3": (ml_dtypes.float8_e4m3fn, 7), "e5m2": (ml_dtypes.float8_e5m2, 14)}[fmt]
    v = np.moveaxis(np.asarray(x, np.float32).astype(ml_dtypes.bfloat16).astype(np.float64), axis, -1)
    blocks = v.reshape(v.shape[:-1] + (-1, 32))
    amax = np.abs(blocks).max(-1, keepdims=True)
    byte = np.maximum(np.where(amax > 0, np.frexp(amax)[1] - 1 + 127, 0) - down, 1)
    scale = np.exp2(byte - 127.0)
    codes = (blocks / scale).astype(np.float32).astype(dtype).astype(np.float64)
    return np.moveaxis((codes * scale).reshape(v.shape), -1, axis)


WIDE = False


def mx_kscale(k):
    if not WIDE:
        return np.ones(k)
    levels = np.array([10, -10, 5, -5, 0])
    if k % 512:
        return np.exp2(np.random.permutation(np.resize(levels, k // 32))).repeat(32)
    a = np.empty((k // 512, 16))
    for p in range(k // 512):
        a[p, :8] = np.random.permutation(np.resize(levels, 8))
        for g in range(8):
            far = levels[np.abs(levels - a[p, g]) >= 10]
            a[p, g + 8] = far[np.random.randint(len(far))]
    return np.exp2(a.ravel()).repeat(32)


def f64(x):
    return np.asarray(x).astype(np.float64)


def striped(idx):
    return np.tile(idx.reshape(-1, 16).T, (8, 1)).astype(np.uint16)


def unstriped(offs):
    return offs[:16].T.reshape(-1).astype(np.int64)


def relu(v):
    return np.maximum(v, 0.0)


K, T, E, C, H, N = 512, 768, 8, 128, 512, 384
TOP = 3
PAD = 64


def by_expert(wq, xq):
    return np.concatenate([wq[e].T @ xq[:, e * C:(e + 1) * C] for e in range(E)], axis=1)


def setup_inputs():
    n = np.random.standard_normal
    s = mx_kscale(K)[:, None]
    u = mx_kscale(H)
    slot_token = np.empty(E * C, np.int64); pos = np.tile(E * C + np.arange(T) % PAD, (TOP, 1)); taken = np.zeros(T, np.int64)
    liked = np.random.randn(T)
    for e in np.random.permutation(E):
        free = np.flatnonzero(taken < TOP); pick = np.random.permutation(free[np.argsort(-(liked[free] + np.random.gumbel(size=free.size)))[:C]]); slot_token[e * C:(e + 1) * C] = pick
        pos[taken[pick], pick] = e * C + np.arange(C); taken[pick] += 1
    g = np.random.uniform(0.2, 0.8, (TOP, T))
    return {
        "xT": (n((K, T)) * s).astype(np.float32),
        "w1": (n((E, K, H)) / np.sqrt(K) / s[None]).astype(np.float32),
        "w3": (n((E, K, H)) / np.sqrt(K) / s[None] * u[None, None, :]).astype(np.float32),
        "w2": (n((E, H, N)) / np.sqrt(H) / u[None, :, None]).astype(np.float32),
        "gate": np.stack([np.tile(r, (N, 1)) for r in g]).astype(np.float32),
        "offs": striped(slot_token),
        "pos1": striped(pos[0]),
        "pos2": striped(pos[1]),
        "pos3": striped(pos[2]),
    }


def reference(xT, w1, w3, w2, gate, offs, pos1, pos2, pos3):
    idx = unstriped(offs)
    xq = mxq(f64(xT)[:, idx], 0, "e4m3")
    h = relu(by_expert(mxq(f64(w1), 1, "e4m3"), xq))
    h = h * by_expert(mxq(f64(w3), 1, "e4m3"), xq)
    y = by_expert(mxq(f64(w2), 1, "e4m3"), mxq(h, 0, "e4m3"))
    y = np.concatenate([y, np.zeros((N, PAD))], axis=1)
    return sum(f64(gate[r]) * y[:, unstriped(p)] for r, p in enumerate((pos1, pos2, pos3)))

@@ -1,0 +1,256 @@
+from contextlib import ExitStack
+
+import concourse.mybir as mybir
+from concourse.masks import make_identity
+
+K, T, E, C, H, N = 512, 768, 8, 128, 512, 384
+TOP = 3
+PAD = 64
+S = E * C
+FLOPS = 2 * S * (2 * K * H + H * N)
+BYTES = 4 * (K * T + 2 * E * K * H + E * H * N + TOP * T + N * T) + 2 * 128 * (S + TOP * T) // 16
+
+F32 = mybir.dt.float32
+BF16 = mybir.dt.bfloat16
+U32 = mybir.dt.uint32
+I32 = mybir.dt.int32
+U16 = mybir.dt.uint16
+U8 = mybir.dt.uint8
+FP8X4 = mybir.dt.float8_e4m3fn_x4
+ACT = mybir.ActivationFunctionType
+ALU = mybir.AluOpType
+
+P = 128
+PACK = 4
+BLOCKS = N // P
+PAIRS = E // 2
+X_PARTS = ((0, 256), (256, 512), (512, 768))
+GATHER = 512
+HALF = T // 2
+CHUNKS = HALF // P
+RAW_BUFS = 12
+W1_SCALAR = 128
+W3_SCALAR = 0
+W3_SCALAR_LAST = 40
+BANKS = {"sums": 3, "turned": 3, "total": 2}
+PIECES = ((0, 512), (512, 768))
+
+
+def tile_moe_ecr_glu_relu_kernel(tc, xT, w1, w3, w2, gate, offs, pos1, pos2, pos3, out):
+    nc = tc.nc
+    with ExitStack() as ctx:
+        keep = ctx.enter_context(tc.tile_pool(name="keep", bufs=1))
+        work = ctx.enter_context(tc.tile_pool(name="work", bufs=3))
+        psum = ctx.enter_context(tc.psum_pool(name="psum", bufs=1))
+
+        def bank(tag):
+            return psum.tile([P, 512], F32, name=tag, tag=tag, bufs=BANKS[tag])
+
+        def turn(tag, shape, dtype):
+            return work.tile(shape, dtype, name=tag, tag=tag, bufs=1, align_bytes=64)
+
+        def copy_on(engine, dst, src):
+            if engine == "v":
+                nc.vector.tensor_copy(out=dst, in_=src)
+            else:
+                nc.scalar.copy(out=dst, in_=src)
+
+        x_scales = keep.tile([P, T], U8, name="x_scales", align_bytes=64)
+        nc.gpsimd.memset(x_scales[:], 0)
+        gate_rows = keep.tile([P, T], F32, name="gate_rows")
+        nc.gpsimd.memset(gate_rows[:], 0.0)
+        ident = keep.tile([P, P], F32, name="ident")
+        make_identity(nc, ident[:])
+        y = [keep.tile([P, S + PAD], F32, name="y%d" % b) for b in range(BLOCKS)]
+        for b in range(BLOCKS):
+            nc.gpsimd.memset(y[b][:, S:], 0.0)
+
+        offs_sb = keep.tile([P, S // 16], U16, name="offs_sb")
+        nc.sync.dma_start(offs_sb[:], offs)
+        x_rows = xT.rearrange("(p j) t -> p j t", j=PACK)
+        x_raw = []
+        for i, (a, z) in enumerate(X_PARTS):
+            part = keep.tile([P, PACK, z - a], F32, name="x_raw%d" % i)
+            nc.sync.dma_start(part[:], x_rows[:, :, a:z])
+            x_raw.append(part)
+
+        nc.sync.dma_start(gate_rows[0:TOP, :], gate[:, 0, :])
+
+        FIRST = 2 * E
+        LOADS = FIRST + BLOCKS * PAIRS
+        raw = {}
+        pos_sb = []
+
+        def slot(n, shape, dtype):
+            return turn("slot%d" % (n % RAW_BUFS), shape, dtype)
+
+        def load(n):
+            if n < FIRST:
+                raw[n] = slot(n, [P, PACK, H], F32)
+                nc.sync.dma_start(raw[n][:], (w1, w3)[n % 2][n // 2].rearrange("(p j) c -> p j c", j=PACK))
+            elif n < LOADS:
+                b, q = divmod(n - FIRST, PAIRS)
+                raw[n] = slot(n, [P, 2, PACK, P], F32)
+                for u in range(2):
+                    rows = w2[2 * q + u].rearrange("(p j) n -> p j n", j=PACK)
+                    nc.sync.dma_start(raw[n][:, u, :, :], rows[:, :, b * P:(b + 1) * P])
+
+        for n in range(RAW_BUFS):
+            load(n)
+            if n == 3:
+                for r, lst in enumerate((pos1, pos2, pos3)):
+                    tile = keep.tile([P, T // 16], U16, name="pos_sb%d" % r)
+                    nc.sync.dma_start(tile[:], lst)
+                    pos_sb.append(tile)
+
+        x_codes = keep.tile([P, T], U32, name="x_codes", align_bytes=64)
+        x_bf = []
+        for i, (a, z) in enumerate(X_PARTS):
+            part = keep.tile([P, (z - a) * PACK], BF16, name="x_bf%d" % i, align_bytes=64)
+            copy_on("vss"[i], part[:].rearrange("p (c i j) -> p c j i", i=4, j=PACK),
+                    x_raw[i][:].rearrange("p j (c i) -> p c j i", i=4))
+            x_bf.append(part)
+        for i, (a, z) in enumerate(X_PARTS):
+            nc.vector.quantize_mx(out=x_codes[:, a:z].bitcast(FP8X4), scales=x_scales[:, a:z], in_=x_bf[i][:])
+        slot_codes, slot_scales = [], []
+
+        def gather_slots(i):
+            cols = slice(i * GATHER // 16, (i + 1) * GATHER // 16)
+            words = keep.tile([P, GATHER], U32, name="slot_codes%d" % i, align_bytes=64)
+            nc.vector.tensor_copy(words[:], x_codes[:].indirect(offs_sb[:, cols]))
+            byts = keep.tile([P, GATHER], U8, name="slot_scales%d" % i, align_bytes=64)
+            nc.vector.tensor_copy(byts[:], x_scales[:].indirect(offs_sb[:, cols]))
+            slot_codes.append(words)
+            slot_scales.append(byts)
+
+        gate_t = keep.tile([P, T // P, TOP], F32, name="gate_t")
+
+        def turn_gate():
+            for h in range(2):
+                turned = bank("sums")
+                for c in range(CHUNKS):
+                    t0 = h * HALF + c * P
+                    nc.tensor.transpose(turned[:, c * P:(c + 1) * P], gate_rows[:, t0:t0 + P], ident[:])
+                nc.scalar.copy(out=gate_t[:, h * CHUNKS:(h + 1) * CHUNKS, :],
+                               in_=turned[:, 0:HALF].rearrange("p (c n) -> p c n", n=P)[:, :, 0:TOP])
+
+        def cast_first(n, scalar_share):
+            rounded = turn("rounded%d" % (n % 4), [P, PACK * H], BF16)
+            dst = rounded[:].rearrange("p (t m j) -> p m j t", t=PACK, j=PACK)
+            src = raw[n][:].rearrange("p j (m t) -> p m j t", t=PACK)
+            if scalar_share > 0:
+                copy_on("s", dst[:, 0:scalar_share], src[:, 0:scalar_share])
+            if scalar_share < P:
+                copy_on("v", dst[:, scalar_share:P], src[:, scalar_share:P])
+            return rounded
+
+        def quantise(src, width, tag=None):
+            if tag is None:
+                codes = work.tile([P, width], U32, name="codes", tag="codes", bufs=4, align_bytes=64)
+            else:
+                codes = turn(tag, [P, width], U32)
+            scales = work.tile([P, width], U8, name="scales", tag="scales", bufs=4, align_bytes=64)
+            nc.vector.quantize_mx(out=codes[:].bitcast(FP8X4), scales=scales[:], in_=src)
+            return codes, scales
+
+        def product_first(wq, e):
+            acc = bank("sums")
+            i, c0 = divmod(e * C, GATHER)
+            for t in range(PACK):
+                nc.tensor.matmul_mx(out=acc[:, t * C:(t + 1) * C],
+                                    lhsT=wq[0][:, t * P:(t + 1) * P].bitcast(FP8X4), lhsT_scale=wq[1][:, t * P:(t + 1) * P],
+                                    rhs=slot_codes[i][:, c0:c0 + C].bitcast(FP8X4), rhs_scale=slot_scales[i][:, c0:c0 + C],
+                                    start=True, stop=True)
+            return acc[:].rearrange("p (t s) -> p s t", t=PACK)
+
+        h_q = []
+        gather_slots(0)
+        def hidden(e, b_sum, relu, tag):
+            h_bf = turn(tag, [P, C * PACK], BF16)
+            nc.vector.tensor_tensor(out=h_bf[:].rearrange("p (s t) -> p s t", t=PACK), in0=b_sum, in1=relu[:], op=ALU.mult)
+            h_codes = keep.tile([P, C], U32, name="h_codes%d" % e, align_bytes=64)
+            h_scales = keep.tile([P, C], U8, name="h_scales%d" % e, align_bytes=64)
+            nc.vector.quantize_mx(out=h_codes[:].bitcast(FP8X4), scales=h_scales[:], in_=h_bf[:])
+            h_q.append((h_codes, h_scales))
+
+        def rectify(a_sum, relu):
+            nc.scalar.activation(out=relu[:], in_=a_sum, func=ACT.Relu)
+            return relu
+
+        a_sum = product_first(quantise(cast_first(0, P)[:], H), 0)
+        load(RAW_BUFS)
+        for e in range(E - 1):
+            b_sum = product_first(quantise(cast_first(2 * e + 1, W3_SCALAR)[:], H), e)
+            load(2 * e + 1 + RAW_BUFS)
+            rounded = cast_first(2 * e + 2, P if e + 2 < E else 64)
+            relu = rectify(a_sum, slot(2 * e + 2, [P, C, PACK], F32))
+            load(2 * e + 2 + RAW_BUFS)
+            a_sum = product_first(quantise(rounded[:], H), e + 1)
+            if e + 2 < E:
+                hidden(e, b_sum, relu, "h_bf")
+            if e == 1:
+                gather_slots(1)
+            if e == 2:
+                turn_gate()
+        rounded = cast_first(FIRST - 1, W3_SCALAR_LAST)
+        last_relu = rectify(a_sum, slot(FIRST - 1, [P, C, PACK], F32))
+        load(FIRST - 1 + RAW_BUFS)
+        last_sum = product_first(quantise(rounded[:], H), E - 1)
+        hidden(E - 2, b_sum, relu, "rounded3")
+        hidden(E - 1, last_sum, last_relu, "h_bf")
+
+        WIDE = 2 * P * PACK
+
+        def second(b, q0, count, engine):
+            rounded = turn("second%d%d" % (b % 2, q0), [P, count * WIDE], BF16)
+            for k in range(count):
+                copy_on(engine, rounded[:, k * WIDE:(k + 1) * WIDE].rearrange("p (u c i j) -> p u c j i", u=2, i=4, j=PACK),
+                        raw[FIRST + b * PAIRS + q0 + k][:].rearrange("p u j (c i) -> p u c j i", i=4))
+            codes, scales = quantise(rounded[:], count * 2 * P)
+            acc = bank("sums")
+            for u in range(2 * count):
+                hc, hs = h_q[2 * q0 + u]
+                nc.tensor.matmul_mx(out=acc[:, u * C:(u + 1) * C],
+                                    lhsT=codes[:, u * P:(u + 1) * P].bitcast(FP8X4), lhsT_scale=scales[:, u * P:(u + 1) * P],
+                                    rhs=hc[:].bitcast(FP8X4), rhs_scale=hs[:], start=True, stop=True)
+            nc.scalar.copy(out=y[b][:, 2 * q0 * C:2 * (q0 + count) * C], in_=acc[:, 0:2 * count * C])
+
+        def combine(b, h, picked, scaled, engine="s"):
+            t0, t1 = PIECES[h]
+            width = t1 - t0
+            for r in range(TOP):
+                nc.vector.tensor_copy(picked[:, r, :], y[b][:].indirect(pos_sb[r][:, t0 // 16:t1 // 16]))
+                turned = bank("turned")
+                for c in range(0, width, P):
+                    nc.tensor.transpose(turned[:, c:c + P], picked[:, r, c:c + P], ident[:])
+                for c in range(0, width, P):
+                    factor = gate_t[:, (t0 + c) // P, r:r + 1]
+                    if engine == "s":
+                        nc.scalar.activation(out=scaled[:, r, c:c + P], in_=turned[:, c:c + P], func=ACT.Copy, scale=factor)
+                    else:
+                        nc.vector.tensor_scalar(out=scaled[:, r, c:c + P], in0=turned[:, c:c + P], scalar1=factor, scalar2=None, op0=ALU.mult)
+            total = bank("total")
+            for c in range(0, width, P):
+                for r in range(TOP):
+                    nc.tensor.matmul(total[:, c:c + P], scaled[:, r, c:c + P], ident[:],
+                                     start=(r == 0), stop=(r == TOP - 1), is_transpose=True)
+            result = work.tile([P, width], F32, name="result", tag="result", bufs=3)
+            copy_on(engine, result[:], total[:, 0:width])
+            nc.sync.dma_start(out[b * P:(b + 1) * P, t0:t1], result[:])
+
+        def three(tag, width):
+            return turn(tag, [P, TOP, width], F32)[:]
+
+        for b in range(2):
+            for q0, count, engine in (((0, 2, "s"), (2, 1, "s"), (3, 1, "v")), ((0, 1, "v"), (1, 2, "s"), (3, 1, "v")))[b]:
+                second(b, q0, count, engine)
+        combine(0, 0, three("picked0", 512), slot(FIRST + PAIRS + 2, [P, TOP, 512], F32)[:])
+        late = three("second13", 256)
+        for q0, count, engine in ((0, 1, "v"), (1, 2, "s"), (3, 1, "v")):
+            second(2, q0, count, engine)
+        both = slot(FIRST + 2 * PAIRS + 2, [P, TOP * T], F32)
+        combine(0, 1, late, both[:, 0:TOP * 256].rearrange("p (r t) -> p r t", r=TOP))
+        combine(1, 0, three("picked1", 512), both[:, TOP * 256:TOP * T].rearrange("p (r t) -> p r t", r=TOP))
+        combine(1, 1, three("second03", 256), three("scaled0", 256))
+        combine(2, 0, three("picked0", 512), three("scaled1", 512))
+        combine(2, 1, three("picked1", 256), three("scaled0", 256), "v")

@@ -13,7 +13,6 @@ BYTES = 4 * (K * T + 2 * E * K * H + E * H * N + TOP * T + N * T) + 2 * 128 * (S
 F32 = mybir.dt.float32
 BF16 = mybir.dt.bfloat16
 U32 = mybir.dt.uint32
-I32 = mybir.dt.int32
 U16 = mybir.dt.uint16
 U8 = mybir.dt.uint8
 FP8X4 = mybir.dt.float8_e4m3fn_x4
@@ -22,134 +21,135 @@ ALU = mybir.AluOpType
 
 P = 128
 PACK = 4
+BANK = 512
 BLOCKS = N // P
-PAIRS = E // 2
-X_PARTS = ((0, 256), (256, 512), (512, 768))
+FIRST = 2 * E
+LOADS = FIRST + BLOCKS * E
+SLOTS = 10
+X_VECTOR = 512
 GATHER = 512
-HALF = T // 2
-CHUNKS = HALF // P
-RAW_BUFS = 12
-W1_SCALAR = 128
 W3_SCALAR = 0
-W3_SCALAR_LAST = 40
-BANKS = {"sums": 3, "turned": 3, "total": 2}
-PIECES = ((0, 512), (512, 768))
+W1_SCALAR_LAST = 64
+W3_SCALAR_LAST = 56
+DIRECT = 384
+BANKS = {"sums": (0, 1, 2, 3), "slots": (0, 1, 2, 3), "turned": (4, 5), "total": (6, 7)}
 
 
 def tile_moe_ecr_glu_relu_kernel(tc, xT, w1, w3, w2, gate, offs, pos1, pos2, pos3, out):
     nc = tc.nc
     with ExitStack() as ctx:
         keep = ctx.enter_context(tc.tile_pool(name="keep", bufs=1))
-        work = ctx.enter_context(tc.tile_pool(name="work", bufs=3))
+        work = ctx.enter_context(tc.tile_pool(name="work", bufs=1))
         psum = ctx.enter_context(tc.psum_pool(name="psum", bufs=1))
+        turns = {}
 
-        def bank(tag):
-            return psum.tile([P, 512], F32, name=tag, tag=tag, bufs=BANKS[tag])
+        def bank(role, again=False):
+            if not again:
+                turns[role] = turns.get(role, -1) + 1
+            name = "bank%d" % BANKS[role][turns[role] % len(BANKS[role])]
+            return psum.tile([P, BANK], F32, name=name, tag=name)
 
-        def turn(tag, shape, dtype):
-            return work.tile(shape, dtype, name=tag, tag=tag, bufs=1, align_bytes=64)
+        def place(tag, shape, dtype, bufs=1):
+            return work.tile(shape, dtype, name=tag, tag=tag, bufs=bufs, align_bytes=64)
+
+        def slot(n):
+            return "slot%d" % (n % SLOTS) if n < FIRST else "part%d" % ((n - FIRST) % 16)
 
         def copy_on(engine, dst, src):
-            if engine == "v":
+            if engine is nc.vector:
                 nc.vector.tensor_copy(out=dst, in_=src)
             else:
                 nc.scalar.copy(out=dst, in_=src)
 
-        x_scales = keep.tile([P, T], U8, name="x_scales", align_bytes=64)
-        nc.gpsimd.memset(x_scales[:], 0)
-        gate_rows = keep.tile([P, T], F32, name="gate_rows")
+        gate_rows = place("rounded2", [P, T], F32)
         nc.gpsimd.memset(gate_rows[:], 0.0)
         ident = keep.tile([P, P], F32, name="ident")
         make_identity(nc, ident[:])
+        x_scales = keep.tile([P, T], U8, name="x_scales", align_bytes=64)
+        nc.gpsimd.memset(x_scales[:], 0)
         y = [keep.tile([P, S + PAD], F32, name="y%d" % b) for b in range(BLOCKS)]
         for b in range(BLOCKS):
             nc.gpsimd.memset(y[b][:, S:], 0.0)
 
         offs_sb = keep.tile([P, S // 16], U16, name="offs_sb")
         nc.sync.dma_start(offs_sb[:], offs)
-        x_rows = xT.rearrange("(p j) t -> p j t", j=PACK)
-        x_raw = []
-        for i, (a, z) in enumerate(X_PARTS):
-            part = keep.tile([P, PACK, z - a], F32, name="x_raw%d" % i)
-            nc.sync.dma_start(part[:], x_rows[:, :, a:z])
-            x_raw.append(part)
-
+        x_raw = place("x_raw", [P, PACK, T], F32)
+        nc.sync.dma_start(x_raw[:], xT.rearrange("(p j) t -> p j t", j=PACK))
         nc.sync.dma_start(gate_rows[0:TOP, :], gate[:, 0, :])
 
-        FIRST = 2 * E
-        LOADS = FIRST + BLOCKS * PAIRS
         raw = {}
-        pos_sb = []
-
-        def slot(n, shape, dtype):
-            return turn("slot%d" % (n % RAW_BUFS), shape, dtype)
 
         def load(n):
             if n < FIRST:
-                raw[n] = slot(n, [P, PACK, H], F32)
+                raw[n] = place(slot(n), [P, PACK, H], F32)
                 nc.sync.dma_start(raw[n][:], (w1, w3)[n % 2][n // 2].rearrange("(p j) c -> p j c", j=PACK))
             elif n < LOADS:
-                b, q = divmod(n - FIRST, PAIRS)
-                raw[n] = slot(n, [P, 2, PACK, P], F32)
-                for u in range(2):
-                    rows = w2[2 * q + u].rearrange("(p j) n -> p j n", j=PACK)
-                    nc.sync.dma_start(raw[n][:, u, :, :], rows[:, :, b * P:(b + 1) * P])
+                b, e = divmod(n - FIRST, E)
+                raw[n] = place(slot(n), [P, PACK, P], F32)
+                nc.sync.dma_start(raw[n][:], w2[e].rearrange("(p j) n -> p j n", j=PACK)[:, :, b * P:(b + 1) * P])
 
-        for n in range(RAW_BUFS):
+        pos_sb = []
+        for n in range(SLOTS):
             load(n)
             if n == 3:
-                for r, lst in enumerate((pos1, pos2, pos3)):
+                for r, positions in enumerate((pos1, pos2, pos3)):
                     tile = keep.tile([P, T // 16], U16, name="pos_sb%d" % r)
-                    nc.sync.dma_start(tile[:], lst)
+                    nc.sync.dma_start(tile[:], positions)
                     pos_sb.append(tile)
 
         x_codes = keep.tile([P, T], U32, name="x_codes", align_bytes=64)
+        x_parts = ((0, X_VECTOR, nc.vector, "rounded3"), (X_VECTOR, T, nc.scalar, "x_bf"))
         x_bf = []
-        for i, (a, z) in enumerate(X_PARTS):
-            part = keep.tile([P, (z - a) * PACK], BF16, name="x_bf%d" % i, align_bytes=64)
-            copy_on("vss"[i], part[:].rearrange("p (c i j) -> p c j i", i=4, j=PACK),
-                    x_raw[i][:].rearrange("p j (c i) -> p c j i", i=4))
+        for t0, t1, engine, tag in x_parts:
+            part = place(tag, [P, (t1 - t0) * PACK], BF16)
+            copy_on(engine, part[:].rearrange("p (c i j) -> p c j i", i=4, j=PACK),
+                    x_raw[:, :, t0:t1].rearrange("p j (c i) -> p c j i", i=4))
             x_bf.append(part)
-        for i, (a, z) in enumerate(X_PARTS):
-            nc.vector.quantize_mx(out=x_codes[:, a:z].bitcast(FP8X4), scales=x_scales[:, a:z], in_=x_bf[i][:])
+        for (t0, t1, engine, tag), part in zip(x_parts, x_bf):
+            nc.vector.quantize_mx(out=x_codes[:, t0:t1].bitcast(FP8X4), scales=x_scales[:, t0:t1], in_=part[:])
         slot_codes, slot_scales = [], []
 
-        def gather_slots(i):
+        def gather_slots(i, tags):
             cols = slice(i * GATHER // 16, (i + 1) * GATHER // 16)
-            words = keep.tile([P, GATHER], U32, name="slot_codes%d" % i, align_bytes=64)
+            words = place(tags[0], [P, GATHER], U32)
             nc.vector.tensor_copy(words[:], x_codes[:].indirect(offs_sb[:, cols]))
-            byts = keep.tile([P, GATHER], U8, name="slot_scales%d" % i, align_bytes=64)
+            byts = place(tags[1], [P, GATHER], U8)
             nc.vector.tensor_copy(byts[:], x_scales[:].indirect(offs_sb[:, cols]))
             slot_codes.append(words)
             slot_scales.append(byts)
 
-        gate_t = keep.tile([P, T // P, TOP], F32, name="gate_t")
+        gather_slots(0, ("slot_codes0", "slot_scales0"))
 
-        def turn_gate():
-            for h in range(2):
-                turned = bank("sums")
-                for c in range(CHUNKS):
-                    t0 = h * HALF + c * P
-                    nc.tensor.transpose(turned[:, c * P:(c + 1) * P], gate_rows[:, t0:t0 + P], ident[:])
-                nc.scalar.copy(out=gate_t[:, h * CHUNKS:(h + 1) * CHUNKS, :],
-                               in_=turned[:, 0:HALF].rearrange("p (c n) -> p c n", n=P)[:, :, 0:TOP])
+        gate_t = keep.tile([P, T // P, TOP], F32, name="gate_t")
+        gate_wide = keep.tile([P, TOP, T], F32, name="gate_wide")
+        for t0 in range(0, T, BANK):
+            t1 = min(t0 + BANK, T)
+            turned = bank("turned")
+            for c in range(t0, t1, P):
+                nc.tensor.transpose(turned[:, c - t0:c - t0 + P], gate_rows[:, c:c + P], ident[:])
+            nc.scalar.copy(out=gate_t[:, t0 // P:t1 // P, :],
+                           in_=turned[:, 0:t1 - t0].rearrange("p (c n) -> p c n", n=P)[:, :, 0:TOP])
+        for r in range(TOP):
+            for t0 in range(0, T, BANK):
+                t1 = min(t0 + BANK, T)
+                spread = bank("total")
+                for c in range(t0, t1, P):
+                    nc.tensor.transpose(spread[:, c - t0:c - t0 + P], gate_t[:, c // P, r:r + 1].to_broadcast([P, P]), ident[:])
+                nc.scalar.copy(out=gate_wide[:, r, t0:t1], in_=spread[:, 0:t1 - t0])
 
         def cast_first(n, scalar_share):
-            rounded = turn("rounded%d" % (n % 4), [P, PACK * H], BF16)
+            rounded = place("rounded%d" % (n % 4), [P, PACK * H], BF16)
             dst = rounded[:].rearrange("p (t m j) -> p m j t", t=PACK, j=PACK)
             src = raw[n][:].rearrange("p j (m t) -> p m j t", t=PACK)
             if scalar_share > 0:
-                copy_on("s", dst[:, 0:scalar_share], src[:, 0:scalar_share])
+                nc.scalar.copy(out=dst[:, 0:scalar_share], in_=src[:, 0:scalar_share])
             if scalar_share < P:
-                copy_on("v", dst[:, scalar_share:P], src[:, scalar_share:P])
+                nc.vector.tensor_copy(out=dst[:, scalar_share:P], in_=src[:, scalar_share:P])
             return rounded
 
         def quantise(src, width, tag=None):
-            if tag is None:
-                codes = work.tile([P, width], U32, name="codes", tag="codes", bufs=4, align_bytes=64)
-            else:
-                codes = turn(tag, [P, width], U32)
-            scales = work.tile([P, width], U8, name="scales", tag="scales", bufs=4, align_bytes=64)
+            codes = place("codes", [P, width], U32, 4) if tag is None else place(tag, [P, width], U32)
+            scales = place("scales", [P, width], U8, 4)
             nc.vector.quantize_mx(out=codes[:].bitcast(FP8X4), scales=scales[:], in_=src)
             return codes, scales
 
@@ -163,94 +163,119 @@ def tile_moe_ecr_glu_relu_kernel(tc, xT, w1, w3, w2, gate, offs, pos1, pos2, pos
                                     start=True, stop=True)
             return acc[:].rearrange("p (t s) -> p s t", t=PACK)
 
+        def rectify(a_sum, tag):
+            relu = place(tag, [P, C, PACK], F32)
+            nc.scalar.activation(out=relu[:], in_=a_sum, func=ACT.Relu)
+            return relu
+
         h_q = []
-        gather_slots(0)
+
         def hidden(e, b_sum, relu, tag):
-            h_bf = turn(tag, [P, C * PACK], BF16)
+            h_bf = place(tag, [P, C * PACK], BF16)
             nc.vector.tensor_tensor(out=h_bf[:].rearrange("p (s t) -> p s t", t=PACK), in0=b_sum, in1=relu[:], op=ALU.mult)
             h_codes = keep.tile([P, C], U32, name="h_codes%d" % e, align_bytes=64)
             h_scales = keep.tile([P, C], U8, name="h_scales%d" % e, align_bytes=64)
             nc.vector.quantize_mx(out=h_codes[:].bitcast(FP8X4), scales=h_scales[:], in_=h_bf[:])
             h_q.append((h_codes, h_scales))
 
-        def rectify(a_sum, relu):
-            nc.scalar.activation(out=relu[:], in_=a_sum, func=ACT.Relu)
-            return relu
+        def load_ahead(n):
+            if n + SLOTS < FIRST:
+                load(n + SLOTS)
+            if n + SLOTS == FIRST - 1:
+                for m in range(FIRST, FIRST + 16):
+                    load(m)
 
-        a_sum = product_first(quantise(cast_first(0, P)[:], H), 0)
-        load(RAW_BUFS)
+        up = cast_first(0, P)
+        load(SLOTS)
+        pending = None
         for e in range(E - 1):
-            b_sum = product_first(quantise(cast_first(2 * e + 1, W3_SCALAR)[:], H), e)
-            load(2 * e + 1 + RAW_BUFS)
-            rounded = cast_first(2 * e + 2, P if e + 2 < E else 64)
-            relu = rectify(a_sum, slot(2 * e + 2, [P, C, PACK], F32))
-            load(2 * e + 2 + RAW_BUFS)
-            a_sum = product_first(quantise(rounded[:], H), e + 1)
-            if e + 2 < E:
-                hidden(e, b_sum, relu, "h_bf")
+            gated = cast_first(2 * e + 1, W3_SCALAR)
+            a_sum = product_first(quantise(up[:], H, slot(2 * e + 1) if e >= 0 else None), e)
+            load_ahead(2 * e + 1)
+            b_sum = product_first(quantise(gated[:], H), e)
+            if pending is not None and e + 2 < E:
+                hidden(*pending, "h_bf")
+            up = cast_first(2 * e + 2, P if e + 2 < E else W1_SCALAR_LAST)
+            before = pending
+            pending = (e, b_sum, rectify(a_sum, slot(2 * e + 2)))
+            load_ahead(2 * e + 2)
             if e == 1:
-                gather_slots(1)
-            if e == 2:
-                turn_gate()
-        rounded = cast_first(FIRST - 1, W3_SCALAR_LAST)
-        last_relu = rectify(a_sum, slot(FIRST - 1, [P, C, PACK], F32))
-        load(FIRST - 1 + RAW_BUFS)
-        last_sum = product_first(quantise(rounded[:], H), E - 1)
-        hidden(E - 2, b_sum, relu, "rounded3")
-        hidden(E - 1, last_sum, last_relu, "h_bf")
+                gather_slots(1, ("slot_codes1", "slot_scales1"))
+        a_sum = product_first(quantise(up[:], H), E - 1)
+        hidden(*before, "rounded2")
+        gated = cast_first(FIRST - 1, W3_SCALAR_LAST)
+        relu = rectify(a_sum, slot(FIRST - 1))
+        b_sum = product_first(quantise(gated[:], H), E - 1)
+        hidden(*pending, "rounded3")
+        hidden(E - 1, b_sum, relu, "h_bf")
 
-        WIDE = 2 * P * PACK
+        def cast_second(b, e0, count, engine, dst):
+            for e in range(e0, e0 + count):
+                copy_on(engine, dst[:, (e % 4) * PACK * P:(e % 4 + 1) * PACK * P].rearrange("p (c i j) -> p c j i", i=4, j=PACK),
+                        raw[FIRST + b * E + e][:].rearrange("p j (c i) -> p c j i", i=4))
+                load(FIRST + b * E + e + 16)
 
-        def second(b, q0, count, engine):
-            rounded = turn("second%d%d" % (b % 2, q0), [P, count * WIDE], BF16)
-            for k in range(count):
-                copy_on(engine, rounded[:, k * WIDE:(k + 1) * WIDE].rearrange("p (u c i j) -> p u c j i", u=2, i=4, j=PACK),
-                        raw[FIRST + b * PAIRS + q0 + k][:].rearrange("p u j (c i) -> p u c j i", i=4))
-            codes, scales = quantise(rounded[:], count * 2 * P)
-            acc = bank("sums")
-            for u in range(2 * count):
-                hc, hs = h_q[2 * q0 + u]
+        def product_second(b, e0, count, src, tag=None):
+            codes, scales = quantise(src[:, (e0 % 4) * PACK * P:(e0 % 4 + count) * PACK * P], count * P, tag)
+            acc = bank("slots")
+            for u in range(count):
+                hc, hs = h_q[e0 + u]
                 nc.tensor.matmul_mx(out=acc[:, u * C:(u + 1) * C],
                                     lhsT=codes[:, u * P:(u + 1) * P].bitcast(FP8X4), lhsT_scale=scales[:, u * P:(u + 1) * P],
                                     rhs=hc[:].bitcast(FP8X4), rhs_scale=hs[:], start=True, stop=True)
-            nc.scalar.copy(out=y[b][:, 2 * q0 * C:2 * (q0 + count) * C], in_=acc[:, 0:2 * count * C])
+            nc.scalar.copy(out=y[b][:, e0 * C:(e0 + count) * C], in_=acc[:, 0:count * C])
 
-        def combine(b, h, picked, scaled, engine="s"):
-            t0, t1 = PIECES[h]
-            width = t1 - t0
+        def weigh(b, t0, t1, tags):
+            parts = []
             for r in range(TOP):
-                nc.vector.tensor_copy(picked[:, r, :], y[b][:].indirect(pos_sb[r][:, t0 // 16:t1 // 16]))
-                turned = bank("turned")
-                for c in range(0, width, P):
-                    nc.tensor.transpose(turned[:, c:c + P], picked[:, r, c:c + P], ident[:])
-                for c in range(0, width, P):
-                    factor = gate_t[:, (t0 + c) // P, r:r + 1]
-                    if engine == "s":
-                        nc.scalar.activation(out=scaled[:, r, c:c + P], in_=turned[:, c:c + P], func=ACT.Copy, scale=factor)
-                    else:
-                        nc.vector.tensor_scalar(out=scaled[:, r, c:c + P], in0=turned[:, c:c + P], scalar1=factor, scalar2=None, op0=ALU.mult)
-            total = bank("total")
+                part = place(tags[r], [P, t1 - t0], F32)
+                nc.vector.tensor_tensor(part[:], y[b][:].indirect(pos_sb[r][:, t0 // 16:t1 // 16]), gate_wide[:, r, t0:t1], ALU.mult)
+                parts.append(part)
+            return parts
+
+        def add_on_tensor(b, t0, t1, parts, behind=False, queue=nc.sync):
+            width = t1 - t0
+            turned = bank("slots", True) if behind else bank("turned")
             for c in range(0, width, P):
                 for r in range(TOP):
-                    nc.tensor.matmul(total[:, c:c + P], scaled[:, r, c:c + P], ident[:],
+                    nc.tensor.matmul(turned[:, c:c + P], parts[r][:, c:c + P], ident[:],
                                      start=(r == 0), stop=(r == TOP - 1), is_transpose=True)
-            result = work.tile([P, width], F32, name="result", tag="result", bufs=3)
-            copy_on(engine, result[:], total[:, 0:width])
-            nc.sync.dma_start(out[b * P:(b + 1) * P, t0:t1], result[:])
+            summed = place("summed", [P, width], F32, 2)
+            nc.scalar.copy(out=summed[:], in_=turned[:, 0:width])
+            total = bank("total")
+            for c in range(0, width, P):
+                nc.tensor.transpose(total[:, c:c + P], summed[:, c:c + P], ident[:])
+            result = place("result", [P, width], F32, 4)
+            nc.scalar.copy(out=result[:], in_=total[:, 0:width])
+            queue.dma_start(out[b * P:(b + 1) * P, t0:t1], result[:])
 
-        def three(tag, width):
-            return turn(tag, [P, TOP, width], F32)[:]
+        def add_on_vector(b, t0, t1, parts):
+            for r in range(1, TOP):
+                nc.vector.tensor_tensor(parts[0][:], parts[0][:], parts[r][:], ALU.add)
+            nc.sync.dma_start(out[b * P:(b + 1) * P, t0:t1], parts[0][:])
 
-        for b in range(2):
-            for q0, count, engine in (((0, 2, "s"), (2, 1, "s"), (3, 1, "v")), ((0, 1, "v"), (1, 2, "s"), (3, 1, "v")))[b]:
-                second(b, q0, count, engine)
-        combine(0, 0, three("picked0", 512), slot(FIRST + PAIRS + 2, [P, TOP, 512], F32)[:])
-        late = three("second13", 256)
-        for q0, count, engine in ((0, 1, "v"), (1, 2, "s"), (3, 1, "v")):
-            second(2, q0, count, engine)
-        both = slot(FIRST + 2 * PAIRS + 2, [P, TOP * T], F32)
-        combine(0, 1, late, both[:, 0:TOP * 256].rearrange("p (r t) -> p r t", r=TOP))
-        combine(1, 0, three("picked1", 512), both[:, TOP * 256:TOP * T].rearrange("p (r t) -> p r t", r=TOP))
-        combine(1, 1, three("second03", 256), three("scaled0", 256))
-        combine(2, 0, three("picked0", 512), three("scaled1", 512))
-        combine(2, 1, three("picked1", 256), three("scaled0", 256), "v")
+        def half(b, k):
+            return place("half%d%d" % (b % 2, k), [P, 4 * PACK * P], BF16)
+
+        halves = [half(0, 0), half(0, 1)]
+        for e0, count, engine in ((0, 2, nc.scalar), (2, 2, nc.scalar), (4, 2, nc.scalar), (6, 1, nc.scalar), (7, 1, nc.vector)):
+            cast_second(0, e0, count, engine, halves[e0 // 4])
+            product_second(0, e0, count, halves[e0 // 4])
+
+        def block(b):
+            halves = [half(b, 0), half(b, 1)]
+            for k in range(2):
+                cast_second(b, 4 * k, 4, nc.scalar, halves[k])
+            product_second(b, 0, 4, halves[0], slot(FIRST + b * E + E - 2))
+            product_second(b, 4, 4, halves[1])
+
+        block(1)
+        add_on_tensor(0, 0, 512, weigh(0, 0, 512, ("a0", "a1", "a2")), True)
+        late = weigh(0, 512, T, ("b0", "half10", "half11"))
+        block(2)
+        add_on_tensor(0, 512, T, late)
+        add_on_tensor(1, 0, 512, weigh(1, 0, 512, ("c0", "c1", "c2")), True)
+        add_on_tensor(1, 512, T, weigh(1, 512, T, ("half00", "half01", "part6")))
+        add_on_tensor(2, 0, DIRECT, weigh(2, 0, DIRECT, ("a0", "a1", "a2")), False, nc.scalar)
+        add_on_vector(2, DIRECT, T - P, weigh(2, DIRECT, T - P, ("c0", "c1", "c2")))
+        add_on_vector(2, T - P, T, weigh(2, T - P, T, ("b0", "half10", "half11")))

from contextlib import ExitStack

import concourse.mybir as mybir
from concourse.masks import make_identity

K, T, E, C, H, N = 512, 768, 8, 128, 512, 384
TOP = 3
PAD = 64
S = E * C
FLOPS = 2 * S * (2 * K * H + H * N)
BYTES = 4 * (K * T + 2 * E * K * H + E * H * N + TOP * T + N * T) + 2 * 128 * (S + TOP * T) // 16

F32 = mybir.dt.float32
BF16 = mybir.dt.bfloat16
U32 = mybir.dt.uint32
U16 = mybir.dt.uint16
U8 = mybir.dt.uint8
FP8X4 = mybir.dt.float8_e4m3fn_x4
ACT = mybir.ActivationFunctionType
ALU = mybir.AluOpType

P = 128
PACK = 4
BANK = 512
BLOCKS = N // P
FIRST = 2 * E
LOADS = FIRST + BLOCKS * E
SLOTS = 10
X_VECTOR = 512
GATHER = 512
W3_SCALAR = 0
W1_SCALAR_LAST = 64
W3_SCALAR_LAST = 56
DIRECT = 384
BANKS = {"sums": (0, 1, 2, 3), "slots": (0, 1, 2, 3), "turned": (4, 5), "total": (6, 7)}


def tile_moe_ecr_glu_relu_kernel(tc, xT, w1, w3, w2, gate, offs, pos1, pos2, pos3, out):
    nc = tc.nc
    with ExitStack() as ctx:
        keep = ctx.enter_context(tc.tile_pool(name="keep", bufs=1))
        work = ctx.enter_context(tc.tile_pool(name="work", bufs=1))
        psum = ctx.enter_context(tc.psum_pool(name="psum", bufs=1))
        turns = {}

        def bank(role, again=False):
            if not again:
                turns[role] = turns.get(role, -1) + 1
            name = "bank%d" % BANKS[role][turns[role] % len(BANKS[role])]
            return psum.tile([P, BANK], F32, name=name, tag=name)

        def place(tag, shape, dtype, bufs=1):
            return work.tile(shape, dtype, name=tag, tag=tag, bufs=bufs, align_bytes=64)

        def slot(n):
            return "slot%d" % (n % SLOTS) if n < FIRST else "part%d" % ((n - FIRST) % 16)

        def copy_on(engine, dst, src):
            if engine is nc.vector:
                nc.vector.tensor_copy(out=dst, in_=src)
            else:
                nc.scalar.copy(out=dst, in_=src)

        gate_rows = place("rounded2", [P, T], F32)
        nc.gpsimd.memset(gate_rows[:], 0.0)
        ident = keep.tile([P, P], F32, name="ident")
        make_identity(nc, ident[:])
        x_scales = keep.tile([P, T], U8, name="x_scales", align_bytes=64)
        nc.gpsimd.memset(x_scales[:], 0)
        y = [keep.tile([P, S + PAD], F32, name="y%d" % b) for b in range(BLOCKS)]
        for b in range(BLOCKS):
            nc.gpsimd.memset(y[b][:, S:], 0.0)

        offs_sb = keep.tile([P, S // 16], U16, name="offs_sb")
        nc.sync.dma_start(offs_sb[:], offs)
        x_raw = place("x_raw", [P, PACK, T], F32)
        nc.sync.dma_start(x_raw[:], xT.rearrange("(p j) t -> p j t", j=PACK))
        nc.sync.dma_start(gate_rows[0:TOP, :], gate[:, 0, :])

        raw = {}

        def load(n):
            if n < FIRST:
                raw[n] = place(slot(n), [P, PACK, H], F32)
                nc.sync.dma_start(raw[n][:], (w1, w3)[n % 2][n // 2].rearrange("(p j) c -> p j c", j=PACK))
            elif n < LOADS:
                b, e = divmod(n - FIRST, E)
                raw[n] = place(slot(n), [P, PACK, P], F32)
                nc.sync.dma_start(raw[n][:], w2[e].rearrange("(p j) n -> p j n", j=PACK)[:, :, b * P:(b + 1) * P])

        pos_sb = []
        for n in range(SLOTS):
            load(n)
            if n == 3:
                for r, positions in enumerate((pos1, pos2, pos3)):
                    tile = keep.tile([P, T // 16], U16, name="pos_sb%d" % r)
                    nc.sync.dma_start(tile[:], positions)
                    pos_sb.append(tile)

        x_codes = keep.tile([P, T], U32, name="x_codes", align_bytes=64)
        x_parts = ((0, X_VECTOR, nc.vector, "rounded3"), (X_VECTOR, T, nc.scalar, "x_bf"))
        x_bf = []
        for t0, t1, engine, tag in x_parts:
            part = place(tag, [P, (t1 - t0) * PACK], BF16)
            copy_on(engine, part[:].rearrange("p (c i j) -> p c j i", i=4, j=PACK),
                    x_raw[:, :, t0:t1].rearrange("p j (c i) -> p c j i", i=4))
            x_bf.append(part)
        for (t0, t1, engine, tag), part in zip(x_parts, x_bf):
            nc.vector.quantize_mx(out=x_codes[:, t0:t1].bitcast(FP8X4), scales=x_scales[:, t0:t1], in_=part[:])
        slot_codes, slot_scales = [], []

        def gather_slots(i, tags):
            cols = slice(i * GATHER // 16, (i + 1) * GATHER // 16)
            words = place(tags[0], [P, GATHER], U32)
            nc.vector.tensor_copy(words[:], x_codes[:].indirect(offs_sb[:, cols]))
            byts = place(tags[1], [P, GATHER], U8)
            nc.vector.tensor_copy(byts[:], x_scales[:].indirect(offs_sb[:, cols]))
            slot_codes.append(words)
            slot_scales.append(byts)

        gather_slots(0, ("slot_codes0", "slot_scales0"))

        gate_t = keep.tile([P, T // P, TOP], F32, name="gate_t")
        gate_wide = keep.tile([P, TOP, T], F32, name="gate_wide")
        for t0 in range(0, T, BANK):
            t1 = min(t0 + BANK, T)
            turned = bank("turned")
            for c in range(t0, t1, P):
                nc.tensor.transpose(turned[:, c - t0:c - t0 + P], gate_rows[:, c:c + P], ident[:])
            nc.scalar.copy(out=gate_t[:, t0 // P:t1 // P, :],
                           in_=turned[:, 0:t1 - t0].rearrange("p (c n) -> p c n", n=P)[:, :, 0:TOP])
        for r in range(TOP):
            for t0 in range(0, T, BANK):
                t1 = min(t0 + BANK, T)
                spread = bank("total")
                for c in range(t0, t1, P):
                    nc.tensor.transpose(spread[:, c - t0:c - t0 + P], gate_t[:, c // P, r:r + 1].to_broadcast([P, P]), ident[:])
                nc.scalar.copy(out=gate_wide[:, r, t0:t1], in_=spread[:, 0:t1 - t0])

        def cast_first(n, scalar_share):
            rounded = place("rounded%d" % (n % 4), [P, PACK * H], BF16)
            dst = rounded[:].rearrange("p (t m j) -> p m j t", t=PACK, j=PACK)
            src = raw[n][:].rearrange("p j (m t) -> p m j t", t=PACK)
            if scalar_share > 0:
                nc.scalar.copy(out=dst[:, 0:scalar_share], in_=src[:, 0:scalar_share])
            if scalar_share < P:
                nc.vector.tensor_copy(out=dst[:, scalar_share:P], in_=src[:, scalar_share:P])
            return rounded

        def quantise(src, width, tag=None):
            codes = place("codes", [P, width], U32, 4) if tag is None else place(tag, [P, width], U32)
            scales = place("scales", [P, width], U8, 4)
            nc.vector.quantize_mx(out=codes[:].bitcast(FP8X4), scales=scales[:], in_=src)
            return codes, scales

        def product_first(wq, e):
            acc = bank("sums")
            i, c0 = divmod(e * C, GATHER)
            for t in range(PACK):
                nc.tensor.matmul_mx(out=acc[:, t * C:(t + 1) * C],
                                    lhsT=wq[0][:, t * P:(t + 1) * P].bitcast(FP8X4), lhsT_scale=wq[1][:, t * P:(t + 1) * P],
                                    rhs=slot_codes[i][:, c0:c0 + C].bitcast(FP8X4), rhs_scale=slot_scales[i][:, c0:c0 + C],
                                    start=True, stop=True)
            return acc[:].rearrange("p (t s) -> p s t", t=PACK)

        def rectify(a_sum, tag):
            relu = place(tag, [P, C, PACK], F32)
            nc.scalar.activation(out=relu[:], in_=a_sum, func=ACT.Relu)
            return relu

        h_q = []

        def hidden(e, b_sum, relu, tag):
            h_bf = place(tag, [P, C * PACK], BF16)
            nc.vector.tensor_tensor(out=h_bf[:].rearrange("p (s t) -> p s t", t=PACK), in0=b_sum, in1=relu[:], op=ALU.mult)
            h_codes = keep.tile([P, C], U32, name="h_codes%d" % e, align_bytes=64)
            h_scales = keep.tile([P, C], U8, name="h_scales%d" % e, align_bytes=64)
            nc.vector.quantize_mx(out=h_codes[:].bitcast(FP8X4), scales=h_scales[:], in_=h_bf[:])
            h_q.append((h_codes, h_scales))

        def load_ahead(n):
            if n + SLOTS < FIRST:
                load(n + SLOTS)
            if n + SLOTS == FIRST - 1:
                for m in range(FIRST, FIRST + 16):
                    load(m)

        up = cast_first(0, P)
        load(SLOTS)
        pending = None
        for e in range(E - 1):
            gated = cast_first(2 * e + 1, W3_SCALAR)
            a_sum = product_first(quantise(up[:], H, slot(2 * e + 1) if e >= 0 else None), e)
            load_ahead(2 * e + 1)
            b_sum = product_first(quantise(gated[:], H), e)
            if pending is not None and e + 2 < E:
                hidden(*pending, "h_bf")
            up = cast_first(2 * e + 2, P if e + 2 < E else W1_SCALAR_LAST)
            before = pending
            pending = (e, b_sum, rectify(a_sum, slot(2 * e + 2)))
            load_ahead(2 * e + 2)
            if e == 1:
                gather_slots(1, ("slot_codes1", "slot_scales1"))
        a_sum = product_first(quantise(up[:], H), E - 1)
        hidden(*before, "rounded2")
        gated = cast_first(FIRST - 1, W3_SCALAR_LAST)
        relu = rectify(a_sum, slot(FIRST - 1))
        b_sum = product_first(quantise(gated[:], H), E - 1)
        hidden(*pending, "rounded3")
        hidden(E - 1, b_sum, relu, "h_bf")

        def cast_second(b, e0, count, engine, dst):
            for e in range(e0, e0 + count):
                copy_on(engine, dst[:, (e % 4) * PACK * P:(e % 4 + 1) * PACK * P].rearrange("p (c i j) -> p c j i", i=4, j=PACK),
                        raw[FIRST + b * E + e][:].rearrange("p j (c i) -> p c j i", i=4))
                load(FIRST + b * E + e + 16)

        def product_second(b, e0, count, src, tag=None):
            codes, scales = quantise(src[:, (e0 % 4) * PACK * P:(e0 % 4 + count) * PACK * P], count * P, tag)
            acc = bank("slots")
            for u in range(count):
                hc, hs = h_q[e0 + u]
                nc.tensor.matmul_mx(out=acc[:, u * C:(u + 1) * C],
                                    lhsT=codes[:, u * P:(u + 1) * P].bitcast(FP8X4), lhsT_scale=scales[:, u * P:(u + 1) * P],
                                    rhs=hc[:].bitcast(FP8X4), rhs_scale=hs[:], start=True, stop=True)
            nc.scalar.copy(out=y[b][:, e0 * C:(e0 + count) * C], in_=acc[:, 0:count * C])

        def weigh(b, t0, t1, tags):
            parts = []
            for r in range(TOP):
                part = place(tags[r], [P, t1 - t0], F32)
                nc.vector.tensor_tensor(part[:], y[b][:].indirect(pos_sb[r][:, t0 // 16:t1 // 16]), gate_wide[:, r, t0:t1], ALU.mult)
                parts.append(part)
            return parts

        def add_on_tensor(b, t0, t1, parts, behind=False, queue=nc.sync):
            width = t1 - t0
            turned = bank("slots", True) if behind else bank("turned")
            for c in range(0, width, P):
                for r in range(TOP):
                    nc.tensor.matmul(turned[:, c:c + P], parts[r][:, c:c + P], ident[:],
                                     start=(r == 0), stop=(r == TOP - 1), is_transpose=True)
            summed = place("summed", [P, width], F32, 2)
            nc.scalar.copy(out=summed[:], in_=turned[:, 0:width])
            total = bank("total")
            for c in range(0, width, P):
                nc.tensor.transpose(total[:, c:c + P], summed[:, c:c + P], ident[:])
            result = place("result", [P, width], F32, 4)
            nc.scalar.copy(out=result[:], in_=total[:, 0:width])
            queue.dma_start(out[b * P:(b + 1) * P, t0:t1], result[:])

        def add_on_vector(b, t0, t1, parts):
            for r in range(1, TOP):
                nc.vector.tensor_tensor(parts[0][:], parts[0][:], parts[r][:], ALU.add)
            nc.sync.dma_start(out[b * P:(b + 1) * P, t0:t1], parts[0][:])

        def half(b, k):
            return place("half%d%d" % (b % 2, k), [P, 4 * PACK * P], BF16)

        halves = [half(0, 0), half(0, 1)]
        for e0, count, engine in ((0, 2, nc.scalar), (2, 2, nc.scalar), (4, 2, nc.scalar), (6, 1, nc.scalar), (7, 1, nc.vector)):
            cast_second(0, e0, count, engine, halves[e0 // 4])
            product_second(0, e0, count, halves[e0 // 4])

        def block(b):
            halves = [half(b, 0), half(b, 1)]
            for k in range(2):
                cast_second(b, 4 * k, 4, nc.scalar, halves[k])
            product_second(b, 0, 4, halves[0], slot(FIRST + b * E + E - 2))
            product_second(b, 4, 4, halves[1])

        block(1)
        add_on_tensor(0, 0, 512, weigh(0, 0, 512, ("a0", "a1", "a2")), True)
        late = weigh(0, 512, T, ("b0", "half10", "half11"))
        block(2)
        add_on_tensor(0, 512, T, late)
        add_on_tensor(1, 0, 512, weigh(1, 0, 512, ("c0", "c1", "c2")), True)
        add_on_tensor(1, 512, T, weigh(1, 512, T, ("half00", "half01", "part6")))
        add_on_tensor(2, 0, DIRECT, weigh(2, 0, DIRECT, ("a0", "a1", "a2")), False, nc.scalar)
        add_on_vector(2, DIRECT, T - P, weigh(2, DIRECT, T - P, ("c0", "c1", "c2")))
        add_on_vector(2, T - P, T, weigh(2, T - P, T, ("b0", "half10", "half11")))
